import numpy as np
import ml_dtypes


def mxq(x, axis, fmt="e4m3"):
    dtype, down = {"e4m3": (ml_dtypes.float8_e4m3fn, 7), "e5m2": (ml_dtypes.float8_e5m2, 14)}[fmt]
    v = np.moveaxis(np.asarray(x, np.float32).astype(ml_dtypes.bfloat16).astype(np.float64), axis, -1)
    blocks = v.reshape(v.shape[:-1] + (-1, 32))
    amax = np.abs(blocks).max(-1, keepdims=True)
    byte = np.maximum(np.where(amax > 0, np.frexp(amax)[1] - 1 + 127, 0) - down, 1)
    scale = np.exp2(byte - 127.0)
    codes = (blocks / scale).astype(np.float32).astype(dtype).astype(np.float64)
    return np.moveaxis((codes * scale).reshape(v.shape), -1, axis)


WIDE = False


def mx_kscale(k):
    if not WIDE:
        return np.ones(k)
    levels = np.array([10, -10, 5, -5, 0])
    if k % 512:
        return np.exp2(np.random.permutation(np.resize(levels, k // 32))).repeat(32)
    a = np.empty((k // 512, 16))
    for p in range(k // 512):
        a[p, :8] = np.random.permutation(np.resize(levels, 8))
        for g in range(8):
            far = levels[np.abs(levels - a[p, g]) >= 10]
            a[p, g + 8] = far[np.random.randint(len(far))]
    return np.exp2(a.ravel()).repeat(32)


BF16 = ml_dtypes.bfloat16


def bf(x):
    return np.asarray(x, np.float32).astype(BF16)


def f64(x):
    return np.asarray(x).astype(np.float64)


E2M1 = np.array([0.0, 0.5, 1.0, 1.5, 2.0, 3.0, 4.0, 6.0, -0.0, -0.5, -1.0, -1.5, -2.0, -3.0, -4.0, -6.0])


def pack_weight(w, fmt):
    k, n = w.shape
    w = f64(bf(w)).reshape(k // 32, 32, n)
    amax = np.abs(w).max(1)
    if fmt == "e4m3":
        byte = np.frexp(amax)[1] - 1 + 127 - 7
    else:
        mant, ex = np.frexp(amax / 6.0)
        byte = np.where(mant > 0.5, ex, ex - 1) + 127
    byte = np.clip(np.where(amax > 0, byte, 1), 1, 254)
    scaled = (w * np.exp2(127.0 - byte)[:, None, :]).reshape(k, n).astype(np.float32)
    by_word = np.ascontiguousarray(scaled.reshape(k // 512, 128, 4, n).transpose(0, 1, 3, 2))
    if fmt == "e4m3":
        words = by_word.astype(ml_dtypes.float8_e4m3fn).view(np.uint8)
    else:
        c = by_word.astype(ml_dtypes.float4_e2m1fn).view(np.uint8) & 0xF
        words = c[..., 0::2] | (c[..., 1::2] << 4)
    return np.ascontiguousarray(words), np.ascontiguousarray(byte.astype(np.uint8).reshape(k // 512, 16, n))


def unpack_weight(words, scales, fmt):
    g, p, n, _ = words.shape
    if fmt == "e4m3":
        vals = np.ascontiguousarray(words).view(ml_dtypes.float8_e4m3fn).astype(np.float64)
    else:
        nib = np.empty((g, p, n, 4), np.uint8)
        nib[..., 0::2] = words & 0xF
        nib[..., 1::2] = words >> 4
        vals = E2M1[nib]
    vals = vals * np.repeat(np.exp2(scales.astype(np.float64) - 127.0), 8, axis=1)[..., None]
    return vals.transpose(0, 1, 3, 2).reshape(g * 512, n)
def pack4(w):
    words, scales = pack_weight(w, "e2m1")
    return words.reshape(words.shape[0], 128, -1), scales


def unpack4(words, scales):
    return unpack_weight(words.reshape(words.shape[0], 128, -1, 2), scales, "e2m1")


def planes(Y):
    n, m = Y.shape
    b = f64(bf(Y)).reshape(n // 32, 32, m)
    amax = np.abs(b).max(1)
    byte = np.clip(np.where(amax > 0, np.frexp(amax)[1] - 1 + 127 - 7, 1), 1, 254)
    codes = (b * np.exp2(127.0 - byte)[:, None, :]).reshape(n, m).astype(np.float32).astype(ml_dtypes.float8_e4m3fn).view(np.uint8)
    words = codes.reshape(n // 512, 128, 4, m).transpose(0, 1, 3, 2)
    return np.ascontiguousarray(words), np.ascontiguousarray(byte.astype(np.uint8).reshape(n // 512, 16, m))


T, K1, K2, N = 2048, 512, 512, 1024


def setup_inputs():
    s1 = mx_kscale(K1)
    s2 = mx_kscale(K2)
    t = mx_kscale(T)
    amp = np.exp(0.6 * np.random.randn(N))
    x = np.random.randn(T, K1)
    r = np.random.randn(T, K2)
    w = 2.0 * amp * np.random.randn(K1, N) / np.sqrt(K1 + K2)
    v = 2.0 * amp * np.random.randn(K2, N) / np.sqrt(K1 + K2)
    v_words, v_scales = pack4(v / s2[:, None])
    left = np.exp(0.3 * np.random.randn(T))
    right = np.exp(0.3 * np.random.randn(T))
    gain = 5.0 * np.exp(0.3 * np.random.randn(N))
    carry = 0.1 * amp * np.random.randn(N, N)
    return {"x": bf(x * s1), "w": bf(w / s1[:, None]),
            "r": bf(r * s2), "v_words": v_words, "v_scales": v_scales,
            "left": bf(left * t), "right": bf(right / t),
            "gain": bf(gain), "carry": bf(carry)}


def reference(x, w, r, v_words, v_scales, left, right, gain, carry):
    xq = mxq(f64(x), 1, "e4m3")
    wq = mxq(f64(w), 0, "e4m3")
    rq = mxq(f64(r), 1, "e4m3")
    v = unpack4(v_words, v_scales)
    z = (xq @ wq) + (rq @ v)
    phi = np.tanh(z) * f64(left)[:, None]
    zr = z * f64(right)[:, None]
    phiq = mxq(phi, 0, "e4m3")
    zq = mxq(zr, 0, "e4m3")
    c = phiq.T @ zq
    y = f64(gain)[:, None] * (np.eye(N) - c / T) + f64(carry)
    words, scales = planes(y.T)
    return y, words, scales

@@ -1,0 +1,488 @@
+from contextlib import ExitStack
+
+import concourse.mybir as mybir
+from concourse.masks import make_identity
+
+T, K, N = 2048, 512, 1024
+FLOPS = 2 * T * 2 * K * N + 2 * T * N * N
+
+F32 = mybir.dt.float32
+BF16 = mybir.dt.bfloat16
+I32 = mybir.dt.int32
+U32 = mybir.dt.uint32
+U8 = mybir.dt.uint8
+FP8X4 = mybir.dt.float8_e4m3fn_x4
+FP4X4 = mybir.dt.float4_e2m1fn_x4
+ACT = mybir.ActivationFunctionType
+ALU = mybir.AluOpType
+
+P = 128
+PACK = 4
+GROUP = P * PACK
+GROUPS = T // GROUP
+BLOCKS = N // P
+HALVES = N // GROUP
+W_CHUNKS = ((0, 512), (512, 1024))
+LAST = GROUPS - 1
+W_TAGS = ("slots", "slots")
+BUFS = {"phi": 8, "slots": 3}
+LATE = 4
+WARM0 = 18
+WARM1 = 8
+WARM2 = 8
+ORDER = (2, 3, 4, 5, 6, 7, 0, 1)
+
+
+def tile_infomax_relative_step_k6_kernel(
+    tc, x, w, r, v_words, v_scales, left, right, gain, carry, out_0, out_1, out_2
+):
+    nc = tc.nc
+    with ExitStack() as ctx:
+        keep = ctx.enter_context(tc.tile_pool(name="keep", bufs=1))
+        work = ctx.enter_context(tc.tile_pool(name="work", bufs=2))
+        acc = ctx.enter_context(tc.psum_pool(name="acc", bufs=5))
+        turn = ctx.enter_context(tc.psum_pool(name="turn", bufs=3))
+        ctx.enter_context(tc.manual_schedule())
+
+        ident = keep.tile([P, P], F32)
+        make_identity(nc, ident[:])
+        zeros = keep.tile([P, GROUP], BF16, align_bytes=64)
+        nc.vector.memset(zeros[:], 0.0)
+        v_plane = keep.tile([P, N], U8, align_bytes=64)
+        nc.vector.memset(v_plane[:].bitcast(I32), 0)
+        warm_codes = keep.tile([P, P], U32, align_bytes=64)
+        warm_scales = keep.tile([P, P], U8, align_bytes=64)
+        nc.vector.quantize_mx(out=warm_codes[:].bitcast(FP8X4), scales=warm_scales[:], in_=zeros[:])
+
+        def warm_up(name, passes):
+            bank = acc.tile([P, P], F32, name=name, tag="acc")
+            for i in range(passes):
+                nc.tensor.matmul_mx(
+                    out=bank[:], lhsT=warm_codes[:].bitcast(FP8X4), lhsT_scale=warm_scales[:],
+                    rhs=warm_codes[:].bitcast(FP8X4), rhs_scale=warm_scales[:], start=True, stop=True,
+                )
+
+        warm_up("warm0", WARM0)
+        warm = keep.tile([P, 1], F32)
+        nc.scalar.activation(out=warm[:], in_=ident[:, 0:1], func=ACT.Tanh)
+
+        raw = {}
+
+        def load_rows(name, src, g):
+            tile = work.tile([P, PACK, K], BF16, name="raw_%s%d" % (name, g), tag="raw", bufs=5)
+            nc.sync.dma_start(out=tile[:], in_=src[g * GROUP : (g + 1) * GROUP, :].rearrange("(p t) k -> p t k", t=PACK))
+            raw[name, g] = tile
+
+        w_raw = {}
+
+        def load_w(i):
+            lo, hi = W_CHUNKS[i]
+            tile = work.tile([P, PACK, hi - lo], BF16, name="w_raw%d" % i, tag=W_TAGS[i], bufs=BUFS[W_TAGS[i]], align_bytes=64)
+            nc.sync.dma_start(out=tile[:], in_=w.rearrange("(p j) n -> p j n", j=PACK)[:, :, lo:hi])
+            w_raw[i] = tile
+
+        load_rows("x", x, 0)
+        load_w(0)
+        load_rows("r", r, 0)
+        v_codes = keep.tile([P, 2 * N], U8, align_bytes=64)
+        nc.sync.dma_start(out=v_codes[:].bitcast(I32), in_=v_words[0].bitcast(I32))
+        for q in range(4):
+            nc.sync.dma_start(
+                out=v_plane[32 * q : 32 * q + 4, :].bitcast(I32),
+                in_=v_scales[0, 4 * q : 4 * q + 4, :].bitcast(I32),
+            )
+        load_w(1)
+        right_sb = keep.tile([P, GROUPS, PACK], BF16)
+        nc.sync.dma_start(out=right_sb[:], in_=right.rearrange("(g p t) -> p g t", p=P, t=PACK))
+        load_rows("x", x, 1)
+        load_rows("r", r, 1)
+        left_sb = keep.tile([P, GROUPS, PACK], BF16)
+        nc.sync.dma_start(out=left_sb[:], in_=left.rearrange("(g p t) -> p g t", p=P, t=PACK))
+        load_rows("x", x, 2)
+
+        w_sorted = {}
+        w_codes = {}
+        w_scales = {}
+
+        def sort_w(i):
+            lo, hi = W_CHUNKS[i]
+            tile = work.tile([P, hi - lo, PACK], BF16, name="w_sorted%d" % i, tag=W_TAGS[i], bufs=BUFS[W_TAGS[i]], align_bytes=64)
+            nc.vector.tensor_copy(
+                out=tile[:].rearrange("p (c i) j -> p c j i", i=4),
+                in_=w_raw[i][:].rearrange("p j (c i) -> p c j i", i=4),
+            )
+            w_sorted[i] = tile
+
+        def quantize_w(i):
+            lo, hi = W_CHUNKS[i]
+            codes = keep.tile([P, hi - lo], U32, name="w_codes%d" % i, align_bytes=64)
+            scales = keep.tile([P, hi - lo], U8, name="w_scales%d" % i, align_bytes=64)
+            nc.vector.quantize_mx(
+                out=codes[:].bitcast(FP8X4), scales=scales[:], in_=w_sorted[i][:].rearrange("p n j -> p (n j)")
+            )
+            for nb in range(lo // P, hi // P):
+                cols = slice(nb * P - lo, (nb + 1) * P - lo)
+                w_codes[nb] = codes[:, cols]
+                w_scales[nb] = scales[:, cols]
+
+        turned = {}
+        in_codes = {}
+        in_scales = {}
+
+        def turn_rows(name, g, h):
+            bank = turn.tile([P, 2, 2, P], F32, name="bank_%s%d%d" % (name, g, h), tag="turn")
+            words = raw[name, g][:].rearrange("p t k -> p (t k)").bitcast(F32)
+            for t in range(2):
+                for u in range(2):
+                    nc.tensor.transpose(bank[:, t, u, :], words[:, 256 * (2 * h + t) + u : 256 * (2 * h + t + 1) : 2], ident[:])
+            tile = work.tile([P, 2 * P * PACK], BF16, name="turned_%s%d%d" % (name, g, h), tag="turned", bufs=4, align_bytes=64)
+            nc.scalar.copy(
+                out=tile[:].bitcast(F32).rearrange("p (t m u) -> p t m u", t=2, u=2),
+                in_=bank[:].rearrange("p t u m -> p t m u"),
+            )
+            turned[name, g, h] = tile
+
+        def quantize_rows(name, g, h):
+            codes = work.tile([P, 2 * P], U32, name="in_codes_%s%d%d" % (name, g, h), tag="in_codes", bufs=8, align_bytes=64)
+            scales = work.tile([P, 2 * P], U8, name="in_scales_%s%d%d" % (name, g, h), tag="in_scales", bufs=8, align_bytes=64)
+            nc.vector.quantize_mx(out=codes[:].bitcast(FP8X4), scales=scales[:], in_=turned[name, g, h][:])
+            for t in range(2):
+                in_codes[name, g, 2 * h + t] = codes[:, t * P : (t + 1) * P]
+                in_scales[name, g, 2 * h + t] = scales[:, t * P : (t + 1) * P]
+
+        score = {}
+        first_group = {}
+        for nb in range(BLOCKS):
+            first_group[nb] = 2 if nb in ORDER[-LATE:] else 0
+            score[nb] = keep.tile([P, GROUPS - first_group[nb], P, PACK], F32, name="score%d" % nb)
+        slot_score = {}
+        for g in range(2):
+            slot_score[g] = keep.tile([P, PACK, LATE, P], F32, name="slot_score%d" % g)
+        z_banks = {}
+        zr = {}
+        zr_codes = {}
+        zr_scales = {}
+
+        def sources(g, nb):
+            bank = acc.tile([P, PACK, P], F32, name="z%d%d" % (g, nb), tag="acc")
+            for t in range(PACK):
+                nc.tensor.matmul_mx(
+                    out=bank[:, t, :],
+                    lhsT=in_codes["x", g, t].bitcast(FP8X4), lhsT_scale=in_scales["x", g, t],
+                    rhs=w_codes[nb].bitcast(FP8X4), rhs_scale=w_scales[nb],
+                    start=True, stop=False,
+                )
+                nc.tensor.matmul_mx(
+                    out=bank[:, t, :],
+                    lhsT=in_codes["r", g, t].bitcast(FP8X4), lhsT_scale=in_scales["r", g, t],
+                    rhs=v_codes[:, 2 * nb * P : 2 * (nb + 1) * P].bitcast(FP4X4),
+                    rhs_scale=v_plane[:, nb * P : (nb + 1) * P],
+                    start=False, stop=True,
+                )
+            if g < first_group[nb]:
+                nc.scalar.activation(out=slot_score[g][:, :, ORDER[-LATE:].index(nb), :], in_=bank[:], func=ACT.Tanh)
+            else:
+                nc.scalar.activation(
+                    out=score[nb][:, g - first_group[nb], :, :], in_=bank[:].rearrange("p t n -> p n t"), func=ACT.Tanh
+                )
+            z_banks[g, nb] = bank
+
+        def weigh_sources(g, nb):
+            half, i = divmod(nb, BLOCKS // HALVES)
+            if i == 0:
+                zr[g, half] = work.tile([P, GROUP, PACK], BF16, name="zr%d%d" % (g, half), tag="zr", bufs=3, align_bytes=64)
+            nc.vector.tensor_tensor(
+                out=zr[g, half][:, i * P : (i + 1) * P, :],
+                in0=z_banks[g, nb][:].rearrange("p t n -> p n t"),
+                in1=right_sb[:, g, :].unsqueeze(1).to_broadcast([P, P, PACK]),
+                op=ALU.mult,
+            )
+
+        def quantize_sources(g, half):
+            codes = keep.tile([P, GROUP], U32, name="zr_codes%d%d" % (g, half), align_bytes=64)
+            scales = keep.tile([P, GROUP], U8, name="zr_scales%d%d" % (g, half), align_bytes=64)
+            nc.vector.quantize_mx(
+                out=codes[:].bitcast(FP8X4), scales=scales[:], in_=zr[g, half][:].rearrange("p n t -> p (n t)")
+            )
+            zr_codes[g, half] = codes
+            zr_scales[g, half] = scales
+
+        phi = {}
+        phi_last = {}
+        phi_codes = {}
+        phi_scales = {}
+
+        def phi_tile(c):
+            if c not in phi:
+                phi[c] = work.tile([P, LAST, P, PACK], BF16, name="phi%d" % c, tag="phi", bufs=BUFS["phi"], align_bytes=64)
+
+        slot_phi = {}
+
+        def weigh_slots(g):
+            slot_phi[g] = work.tile([P, PACK, LATE, P], BF16, name="slot_phi%d" % g, tag="slots", bufs=BUFS["slots"], align_bytes=64)
+            for t in range(PACK):
+                nc.scalar.activation(
+                    out=slot_phi[g][:, t, :, :], in_=slot_score[g][:, t, :, :], func=ACT.Copy, scale=left32[:, g, t : t + 1]
+                )
+
+        def sort_slots(c, g):
+            phi_tile(c)
+            nc.scalar.copy(
+                out=phi[c][:, g, :, :].rearrange("p (n i) t -> p n t i", i=4),
+                in_=slot_phi[g][:, :, ORDER[-LATE:].index(c), :].rearrange("p t (n i) -> p n t i", i=4),
+            )
+
+        def weigh_score(engine, c, lo, hi):
+            phi_tile(c)
+            engine.tensor_tensor(
+                out=phi[c][:, lo:hi, :, :],
+                in0=score[c][:, lo - first_group[c] : hi - first_group[c], :, :],
+                in1=left_sb[:, lo:hi, :].unsqueeze(2).to_broadcast([P, hi - lo, P, PACK]),
+                op=ALU.mult,
+            )
+
+        def weigh_last_score(c, tag, bufs):
+            phi_last[c] = work.tile([P, P, PACK], BF16, name="phi_last%d" % c, tag=tag, bufs=bufs, align_bytes=64)
+            nc.gpsimd.tensor_tensor(
+                out=phi_last[c][:],
+                in0=score[c][:, LAST - first_group[c], :, :],
+                in1=left_sb[:, LAST, :].unsqueeze(1).to_broadcast([P, P, PACK]),
+                op=ALU.mult,
+            )
+
+        def quantize_score(c):
+            phi_codes[c] = work.tile([P, GROUPS * P], U32, name="phi_codes%d" % c, tag="phi_codes", bufs=4, align_bytes=64)
+            phi_scales[c] = work.tile([P, GROUPS * P], U8, name="phi_scales%d" % c, tag="phi_scales", bufs=4, align_bytes=64)
+            flat = phi[c][:].rearrange("p g n t -> p (g n t)")
+            for lo, hi in ((0, 2), (2, 3)):
+                nc.vector.quantize_mx(
+                    out=phi_codes[c][:, lo * P : hi * P].bitcast(FP8X4), scales=phi_scales[c][:, lo * P : hi * P],
+                    in_=flat[:, lo * GROUP : hi * GROUP],
+                )
+
+        def quantize_last_score(c):
+            nc.vector.quantize_mx(
+                out=phi_codes[c][:, LAST * P :].bitcast(FP8X4), scales=phi_scales[c][:, LAST * P :],
+                in_=phi_last[c][:].rearrange("p n t -> p (n t)"),
+            )
+
+        c_banks = {}
+
+        def correlate(c, half, lo, hi):
+            if lo == 0:
+                c_banks[c, half] = acc.tile([P, GROUP], F32, name="c%d%d" % (c, half), tag="acc")
+            for g in range(lo, hi):
+                cols = slice(g * P, (g + 1) * P)
+                nc.tensor.matmul_mx(
+                    out=c_banks[c, half][:],
+                    lhsT=phi_codes[c][:, cols].bitcast(FP8X4), lhsT_scale=phi_scales[c][:, cols],
+                    rhs=zr_codes[g, half][:].bitcast(FP8X4), rhs_scale=zr_scales[g, half][:],
+                    start=(g == 0), stop=(g == LAST),
+                )
+
+        y = {}
+        y_rows = {}
+        carry_sb = {}
+
+        def finish(c, half):
+            if c not in y_rows:
+                y_rows[c] = work.tile([P, N], F32, name="y%d" % c, tag="raw", bufs=5)
+            y[c, half] = y_rows[c][:, half * GROUP : (half + 1) * GROUP]
+            nc.vector.scalar_tensor_tensor(
+                out=y[c, half], in0=c_banks[c, half][:], scalar=minus_gain[:, c : c + 1],
+                in1=carry_sb[c // 2][:, c % 2, half * GROUP : (half + 1) * GROUP],
+                op0=ALU.mult, op1=ALU.add,
+            )
+
+        def add_diagonal(c):
+            half, i = divmod(c, BLOCKS // HALVES)
+            block = y[c, half][:, i * P : (i + 1) * P]
+            nc.vector.scalar_tensor_tensor(
+                out=block, in0=ident[:], scalar=gain_sb[:, c : c + 1], in1=block, op0=ALU.mult, op1=ALU.add
+            )
+            nc.sync.dma_start(out=out_0[c * P : (c + 1) * P, :], in_=y_rows[c][:])
+
+        y_sorted = {}
+        y_turned = {}
+
+        def round_y(c, half, copy):
+            y_sorted[c, half] = work.tile([P, GROUP], BF16, name="y_sorted%d%d" % (c, half), tag="y_sorted", bufs=6)
+            copy(
+                out=y_sorted[c, half][:].rearrange("m (u p e) -> m u p e", u=2, e=2),
+                in_=y[c, half].rearrange("m (p u e) -> m u p e", u=2, e=2),
+            )
+
+        def turn_y(c, halves, copy):
+            bank = turn.tile([P, len(halves), 2, P], F32, name="bank_y%d%d" % (c, halves[0]), tag="turn")
+            for i, half in enumerate(halves):
+                words = y_sorted[c, half][:].bitcast(F32)
+                for u in range(2):
+                    nc.tensor.transpose(bank[:, i, u, :], words[:, u * P : (u + 1) * P], ident[:])
+            tile = work.tile([P, len(halves) * GROUP], BF16, name="y_turned%d%d" % (c, halves[0]), tag="turned", bufs=4, align_bytes=64)
+            copy(
+                out=tile[:].bitcast(F32).rearrange("p (h m u) -> p h m u", h=len(halves), u=2),
+                in_=bank[:].rearrange("p h u m -> p h m u"),
+            )
+            for i, half in enumerate(halves):
+                y_turned[c, half] = tile[:, i * GROUP : (i + 1) * GROUP]
+
+        y_scales = keep.tile([P, HALVES, N], U8, align_bytes=64)
+
+        y_codes = keep.tile([P, HALVES, N], U32, align_bytes=64)
+
+        def quantize_y(c, halves):
+            for half in halves:
+                nc.vector.quantize_mx(
+                    out=y_codes[:, half, c * P : (c + 1) * P].bitcast(FP8X4),
+                    scales=y_scales[:, half, c * P : (c + 1) * P],
+                    in_=y_turned[c, half],
+                )
+
+        def store_codes(lo, hi):
+            nc.sync.dma_start(
+                out=out_1[:, :, lo * P : hi * P, :].rearrange("h p m t -> p h (m t)").bitcast(I32),
+                in_=y_codes[:, :, lo * P : hi * P].bitcast(I32),
+            )
+
+        turn_rows("x", 0, 0)
+        turn_rows("x", 0, 1)
+        warm_up("warm1", WARM1)
+        turn_rows("r", 0, 0)
+        turn_rows("r", 0, 1)
+        warm_up("warm2", WARM2)
+        sort_w(0)
+        quantize_rows("x", 0, 0)
+        quantize_rows("x", 0, 1)
+        quantize_w(0)
+        quantize_rows("r", 0, 0)
+        quantize_rows("r", 0, 1)
+        sort_w(1)
+
+        load_rows("r", r, 2)
+        load_rows("x", x, LAST)
+        gain_raw = keep.tile([P, BLOCKS, 2], BF16)
+
+        def load_rest():
+            load_rows("r", r, LAST)
+            with nc.allow_non_contiguous_dma(reason="one gain to a partition"):
+                nc.sync.dma_start(out=gain_raw[:, :, 0], in_=gain.rearrange("(c p) -> p c", p=P))
+            for i in range(BLOCKS // 2):
+                carry_sb[i] = keep.tile([P, 2, N], BF16, name="carry%d" % i)
+                nc.sync.dma_start(
+                    out=carry_sb[i][:], in_=carry[2 * i * P : 2 * (i + 1) * P, :].rearrange("(c p) n -> p c n", p=P)
+                )
+
+        left32 = keep.tile([P, GROUPS, PACK], F32)
+        gain_sb = keep.tile([P, BLOCKS], F32)
+        minus_gain = keep.tile([P, BLOCKS], F32)
+
+        for g in range(GROUPS):
+            turn_at = 2 if g == 0 else 0
+            for nb in range(BLOCKS):
+                sources(g, nb)
+                weigh_sources(g, nb)
+                if g == 0:
+                    if nb == 0:
+                        quantize_w(1)
+                    if nb == 2:
+                        weigh_score(nc.vector, ORDER[0], g, g + 1)
+                    if nb == 4:
+                        weigh_score(nc.gpsimd, ORDER[2], g, g + 1)
+                        weigh_score(nc.gpsimd, ORDER[1], g, g + 1)
+                elif nb in ORDER[:3]:
+                    if g < LAST:
+                        weigh_score(nc.gpsimd, nb, g, g + 1)
+                    elif nb == ORDER[2]:
+                        weigh_last_score(nb, "phi_late", 1)
+                    else:
+                        weigh_last_score(nb, "phi_early", 2)
+                if nb == 0 and g > 0:
+                    quantize_sources(g - 1, 0)
+                    quantize_sources(g - 1, 1)
+                    weigh_score(nc.vector, ORDER[3], g - 1, g)
+                if nb == 0 and g == 1:
+                    nc.vector.tensor_copy(out=left32[:], in_=left_sb[:])
+                if nb == 4 and g == LAST:
+                    weigh_slots(0)
+                if turn_at <= nb < turn_at + 2 and g < LAST:
+                    name = ("x", "r")[nb - turn_at]
+                    turn_rows(name, g + 1, 0)
+                    turn_rows(name, g + 1, 1)
+                    quantize_rows(name, g + 1, 0)
+                    quantize_rows(name, g + 1, 1)
+                    if g == 0 and name == "x":
+                        load_rest()
+                if nb == 0 and g == LAST:
+                    quantize_score(ORDER[0])
+                    quantize_score(ORDER[1])
+                    nc.vector.tensor_copy(out=gain_sb[:], in_=gain_raw[:, :, 0])
+                    nc.vector.tensor_scalar(
+                        out=minus_gain[:], in0=gain_raw[:, :, 0], scalar1=-1.0 / T, scalar2=None, op0=ALU.mult
+                    )
+
+        weigh_slots(1)
+        correlate(ORDER[0], 0, 0, LAST)
+        correlate(ORDER[0], 1, 0, LAST)
+        correlate(ORDER[1], 0, 0, LAST)
+        quantize_sources(LAST, 0)
+        quantize_last_score(ORDER[0])
+        correlate(ORDER[0], 0, LAST, GROUPS)
+        quantize_sources(LAST, 1)
+        correlate(ORDER[0], 1, LAST, GROUPS)
+        quantize_last_score(ORDER[1])
+        correlate(ORDER[1], 0, LAST, GROUPS)
+        correlate(ORDER[1], 1, 0, GROUPS)
+        quantize_score(ORDER[2])
+        quantize_last_score(ORDER[2])
+        both = (0, 1)
+        for i in range(BLOCKS - 2):
+            if i + 4 < BLOCKS:
+                sort_slots(ORDER[i + 4], 0)
+                sort_slots(ORDER[i + 4], 1)
+            if i + 3 < BLOCKS:
+                weigh_last_score(ORDER[i + 3], "phi_late", 1)
+            c = ORDER[i]
+            first = c // (BLOCKS // HALVES)
+            finish(c, first)
+            finish(c, 1 - first)
+            add_diagonal(c)
+            if i >= 1:
+                turn_y(ORDER[i - 1], both, nc.scalar.copy)
+            if i + 2 < BLOCKS:
+                correlate(ORDER[i + 2], 0, 0, GROUPS)
+                correlate(ORDER[i + 2], 1, 0, GROUPS)
+            round_y(c, 1 - first, nc.scalar.copy)
+            round_y(c, first, nc.scalar.copy)
+            if i + 4 < BLOCKS:
+                weigh_score(nc.vector, ORDER[i + 4], 2, LAST)
+            if i >= 2:
+                quantize_y(ORDER[i - 2], both)
+                if i % 2 == 1:
+                    store_codes(ORDER[i - 3], ORDER[i - 2] + 1)
+            if i + 3 < BLOCKS:
+                quantize_score(ORDER[i + 3])
+                quantize_last_score(ORDER[i + 3])
+        for c, copy in ((ORDER[-2], nc.scalar.copy), (ORDER[-1], nc.vector.tensor_copy)):
+            first = c // (BLOCKS // HALVES)
+            finish(c, first)
+            finish(c, 1 - first)
+            add_diagonal(c)
+            round_y(c, 1 - first, copy)
+            round_y(c, first, copy)
+        turn_y(ORDER[-3], both, nc.scalar.copy)
+        turn_y(ORDER[-2], both, nc.scalar.copy)
+        quantize_y(ORDER[-4], both)
+        quantize_y(ORDER[-3], both)
+        store_codes(ORDER[-4], ORDER[-3] + 1)
+        turn_y(c, (1 - first,), nc.scalar.copy)
+        turn_y(c, (first,), nc.vector.tensor_copy)
+        quantize_y(ORDER[-2], both)
+        store_codes(ORDER[-2], ORDER[-2] + 1)
+        quantize_y(c, (1 - first,))
+        quantize_y(c, (first,))
+        store_codes(c, c + 1)
+        for q in range(4):
+            (nc.sync, nc.scalar)[q % 2].dma_start(
+                out=out_2[:, 4 * q : 4 * q + 4, :].rearrange("h r m -> r h m").bitcast(I32),
+                in_=y_scales[32 * q : 32 * q + 4, :, :].bitcast(I32),
+            )

@@ -26,8 +26,13 @@ W_CHUNKS = ((0, 512), (512, 1024))
 LAST = GROUPS - 1
 W_TAGS = ("slots", "slots")
 BUFS = {"phi": 8, "slots": 3}
-LATE = 4
-WARM0 = 18
+LATE = 5
+RUN16 = False
+TURN0 = 2
+SLOTNB = 1
+FIRST = (2, 3, 0, 1, 4, 5, 6, 7)
+PAIR = False
+WARM0 = 16
 WARM1 = 8
 WARM2 = 8
 ORDER = (2, 3, 4, 5, 6, 7, 0, 1)
@@ -40,8 +45,8 @@ def tile_infomax_relative_step_k6_kernel(
     with ExitStack() as ctx:
         keep = ctx.enter_context(tc.tile_pool(name="keep", bufs=1))
         work = ctx.enter_context(tc.tile_pool(name="work", bufs=2))
-        acc = ctx.enter_context(tc.psum_pool(name="acc", bufs=5))
-        turn = ctx.enter_context(tc.psum_pool(name="turn", bufs=3))
+        acc = ctx.enter_context(tc.psum_pool(name="acc", bufs=4 if RUN16 else 5))
+        turn = ctx.enter_context(tc.psum_pool(name="turn", bufs=4 if RUN16 else 3))
         ctx.enter_context(tc.manual_schedule())
 
         ident = keep.tile([P, P], F32)
@@ -91,13 +96,13 @@ def tile_infomax_relative_step_k6_kernel(
                 out=v_plane[32 * q : 32 * q + 4, :].bitcast(I32),
                 in_=v_scales[0, 4 * q : 4 * q + 4, :].bitcast(I32),
             )
-        load_w(1)
         right_sb = keep.tile([P, GROUPS, PACK], BF16)
         nc.sync.dma_start(out=right_sb[:], in_=right.rearrange("(g p t) -> p g t", p=P, t=PACK))
-        load_rows("x", x, 1)
-        load_rows("r", r, 1)
+        load_w(1)
         left_sb = keep.tile([P, GROUPS, PACK], BF16)
         nc.sync.dma_start(out=left_sb[:], in_=left.rearrange("(g p t) -> p g t", p=P, t=PACK))
+        load_rows("x", x, 1)
+        load_rows("r", r, 1)
         load_rows("x", x, 2)
 
         w_sorted = {}
@@ -107,10 +112,9 @@ def tile_infomax_relative_step_k6_kernel(
         def sort_w(i):
             lo, hi = W_CHUNKS[i]
             tile = work.tile([P, hi - lo, PACK], BF16, name="w_sorted%d" % i, tag=W_TAGS[i], bufs=BUFS[W_TAGS[i]], align_bytes=64)
-            nc.vector.tensor_copy(
-                out=tile[:].rearrange("p (c i) j -> p c j i", i=4),
-                in_=w_raw[i][:].rearrange("p j (c i) -> p c j i", i=4),
-            )
+            out = tile[:].rearrange("p (c i) j -> p c j i", i=4)
+            in_ = w_raw[i][:].rearrange("p j (c i) -> p c j i", i=4)
+            nc.vector.tensor_copy(out=out, in_=in_)
             w_sorted[i] = tile
 
         def quantize_w(i):
@@ -135,20 +139,21 @@ def tile_infomax_relative_step_k6_kernel(
             for t in range(2):
                 for u in range(2):
                     nc.tensor.transpose(bank[:, t, u, :], words[:, 256 * (2 * h + t) + u : 256 * (2 * h + t + 1) : 2], ident[:])
-            tile = work.tile([P, 2 * P * PACK], BF16, name="turned_%s%d%d" % (name, g, h), tag="turned", bufs=4, align_bytes=64)
+            if h == 0:
+                turned[name, g] = work.tile([P, GROUP * PACK], BF16, name="turned_%s%d" % (name, g), tag="turned", bufs=2, align_bytes=64)
+                in_codes[name, g] = work.tile([P, GROUP], U32, name="in_codes_%s%d" % (name, g), tag="in_codes", bufs=4, align_bytes=64)
+                in_scales[name, g] = work.tile([P, GROUP], U8, name="in_scales_%s%d" % (name, g), tag="in_scales", bufs=4, align_bytes=64)
             nc.scalar.copy(
-                out=tile[:].bitcast(F32).rearrange("p (t m u) -> p t m u", t=2, u=2),
+                out=turned[name, g][:, 2 * h * GROUP : 2 * (h + 1) * GROUP].bitcast(F32).rearrange("p (t m u) -> p t m u", t=2, u=2),
                 in_=bank[:].rearrange("p t u m -> p t m u"),
             )
-            turned[name, g, h] = tile
 
-        def quantize_rows(name, g, h):
-            codes = work.tile([P, 2 * P], U32, name="in_codes_%s%d%d" % (name, g, h), tag="in_codes", bufs=8, align_bytes=64)
-            scales = work.tile([P, 2 * P], U8, name="in_scales_%s%d%d" % (name, g, h), tag="in_scales", bufs=8, align_bytes=64)
-            nc.vector.quantize_mx(out=codes[:].bitcast(FP8X4), scales=scales[:], in_=turned[name, g, h][:])
-            for t in range(2):
-                in_codes[name, g, 2 * h + t] = codes[:, t * P : (t + 1) * P]
-                in_scales[name, g, 2 * h + t] = scales[:, t * P : (t + 1) * P]
+        def quantize_rows(name, g, lo, hi):
+            cols = slice(2 * lo * P, 2 * hi * P)
+            nc.vector.quantize_mx(
+                out=in_codes[name, g][:, cols].bitcast(FP8X4), scales=in_scales[name, g][:, cols],
+                in_=turned[name, g][:, 2 * lo * GROUP : 2 * hi * GROUP],
+            )
 
         score = {}
         first_group = {}
@@ -166,15 +171,16 @@ def tile_infomax_relative_step_k6_kernel(
         def sources(g, nb):
             bank = acc.tile([P, PACK, P], F32, name="z%d%d" % (g, nb), tag="acc")
             for t in range(PACK):
+                cols = slice(t * P, (t + 1) * P)
                 nc.tensor.matmul_mx(
                     out=bank[:, t, :],
-                    lhsT=in_codes["x", g, t].bitcast(FP8X4), lhsT_scale=in_scales["x", g, t],
+                    lhsT=in_codes["x", g][:, cols].bitcast(FP8X4), lhsT_scale=in_scales["x", g][:, cols],
                     rhs=w_codes[nb].bitcast(FP8X4), rhs_scale=w_scales[nb],
                     start=True, stop=False,
                 )
                 nc.tensor.matmul_mx(
                     out=bank[:, t, :],
-                    lhsT=in_codes["r", g, t].bitcast(FP8X4), lhsT_scale=in_scales["r", g, t],
+                    lhsT=in_codes["r", g][:, cols].bitcast(FP8X4), lhsT_scale=in_scales["r", g][:, cols],
                     rhs=v_codes[:, 2 * nb * P : 2 * (nb + 1) * P].bitcast(FP4X4),
                     rhs_scale=v_plane[:, nb * P : (nb + 1) * P],
                     start=False, stop=True,
@@ -189,7 +195,7 @@ def tile_infomax_relative_step_k6_kernel(
 
         def weigh_sources(g, nb):
             half, i = divmod(nb, BLOCKS // HALVES)
-            if i == 0:
+            if (g, half) not in zr:
                 zr[g, half] = work.tile([P, GROUP, PACK], BF16, name="zr%d%d" % (g, half), tag="zr", bufs=3, align_bytes=64)
             nc.vector.tensor_tensor(
                 out=zr[g, half][:, i * P : (i + 1) * P, :],
@@ -218,9 +224,10 @@ def tile_infomax_relative_step_k6_kernel(
 
         slot_phi = {}
 
-        def weigh_slots(g):
-            slot_phi[g] = work.tile([P, PACK, LATE, P], BF16, name="slot_phi%d" % g, tag="slots", bufs=BUFS["slots"], align_bytes=64)
-            for t in range(PACK):
+        def weigh_slots(g, slots):
+            if g not in slot_phi:
+              slot_phi[g] = work.tile([P, PACK, LATE, P], BF16, name="slot_phi%d" % g, tag="slots", bufs=BUFS["slots"], align_bytes=64)
+            for t in slots:
                 nc.scalar.activation(
                     out=slot_phi[g][:, t, :, :], in_=slot_score[g][:, t, :, :], func=ACT.Copy, scale=left32[:, g, t : t + 1]
                 )
@@ -250,11 +257,13 @@ def tile_infomax_relative_step_k6_kernel(
                 op=ALU.mult,
             )
 
-        def quantize_score(c):
+        def quantize_score(c, parts=((0, 2), (2, 3))):
+          if c not in phi_codes:
             phi_codes[c] = work.tile([P, GROUPS * P], U32, name="phi_codes%d" % c, tag="phi_codes", bufs=4, align_bytes=64)
             phi_scales[c] = work.tile([P, GROUPS * P], U8, name="phi_scales%d" % c, tag="phi_scales", bufs=4, align_bytes=64)
+          if True:
             flat = phi[c][:].rearrange("p g n t -> p (g n t)")
-            for lo, hi in ((0, 2), (2, 3)):
+            for lo, hi in parts:
                 nc.vector.quantize_mx(
                     out=phi_codes[c][:, lo * P : hi * P].bitcast(FP8X4), scales=phi_scales[c][:, lo * P : hi * P],
                     in_=flat[:, lo * GROUP : hi * GROUP],
@@ -318,7 +327,7 @@ def tile_infomax_relative_step_k6_kernel(
                 words = y_sorted[c, half][:].bitcast(F32)
                 for u in range(2):
                     nc.tensor.transpose(bank[:, i, u, :], words[:, u * P : (u + 1) * P], ident[:])
-            tile = work.tile([P, len(halves) * GROUP], BF16, name="y_turned%d%d" % (c, halves[0]), tag="turned", bufs=4, align_bytes=64)
+            tile = work.tile([P, len(halves) * GROUP], BF16, name="y_turned%d%d" % (c, halves[0]), tag="y_turned", bufs=4, align_bytes=64)
             copy(
                 out=tile[:].bitcast(F32).rearrange("p (h m u) -> p h m u", h=len(halves), u=2),
                 in_=bank[:].rearrange("p h u m -> p h m u"),
@@ -351,11 +360,10 @@ def tile_infomax_relative_step_k6_kernel(
         turn_rows("r", 0, 1)
         warm_up("warm2", WARM2)
         sort_w(0)
-        quantize_rows("x", 0, 0)
-        quantize_rows("x", 0, 1)
+        quantize_rows("x", 0, 0, 2)
         quantize_w(0)
-        quantize_rows("r", 0, 0)
-        quantize_rows("r", 0, 1)
+        quantize_rows("r", 0, 0, 1)
+        quantize_rows("r", 0, 1, 2)
         sort_w(1)
 
         load_rows("r", r, 2)
@@ -377,15 +385,16 @@ def tile_infomax_relative_step_k6_kernel(
         minus_gain = keep.tile([P, BLOCKS], F32)
 
         for g in range(GROUPS):
-            turn_at = 2 if g == 0 else 0
+            turn_at = TURN0 if g == 0 else 0
             for nb in range(BLOCKS):
-                sources(g, nb)
-                weigh_sources(g, nb)
+                block = FIRST[nb] if g == 0 else nb
+                sources(g, block)
+                weigh_sources(g, block)
                 if g == 0:
                     if nb == 0:
-                        quantize_w(1)
+                        weigh_score(nc.gpsimd, ORDER[0], g, g + 1)
                     if nb == 2:
-                        weigh_score(nc.vector, ORDER[0], g, g + 1)
+                        quantize_w(1)
                     if nb == 4:
                         weigh_score(nc.gpsimd, ORDER[2], g, g + 1)
                         weigh_score(nc.gpsimd, ORDER[1], g, g + 1)
@@ -399,41 +408,59 @@ def tile_infomax_relative_step_k6_kernel(
                 if nb == 0 and g > 0:
                     quantize_sources(g - 1, 0)
                     quantize_sources(g - 1, 1)
-                    weigh_score(nc.vector, ORDER[3], g - 1, g)
-                if nb == 0 and g == 1:
+                if nb == 0 and g == 2:
+                    quantize_score(ORDER[0], ((0, 2),))
+                    quantize_score(ORDER[1], ((0, 2),))
+                if nb == 3 and g == 0:
                     nc.vector.tensor_copy(out=left32[:], in_=left_sb[:])
                 if nb == 4 and g == LAST:
-                    weigh_slots(0)
-                if turn_at <= nb < turn_at + 2 and g < LAST:
+                    weigh_slots(0, (2, 3))
+                if nb == SLOTNB and g in (1, 2):
+                    weigh_slots(0, (g - 1,))
+                if LATE == 4 and nb == 0 and g in (1, 2):
+                    weigh_score(nc.vector, ORDER[3], g - 1, g)
+                if RUN16 and nb == turn_at and g < LAST:
+                    for name in ("x", "r"):
+                        turn_rows(name, g + 1, 0)
+                        turn_rows(name, g + 1, 1)
+                    for name in ("x", "r"):
+                        quantize_rows(name, g + 1, 0, 2)
+                    if g == 0:
+                        load_rest()
+                if not RUN16 and turn_at <= nb < turn_at + 2 and g < LAST:
                     name = ("x", "r")[nb - turn_at]
                     turn_rows(name, g + 1, 0)
                     turn_rows(name, g + 1, 1)
-                    quantize_rows(name, g + 1, 0)
-                    quantize_rows(name, g + 1, 1)
+                    quantize_rows(name, g + 1, 0, 2)
                     if g == 0 and name == "x":
                         load_rest()
                 if nb == 0 and g == LAST:
-                    quantize_score(ORDER[0])
-                    quantize_score(ORDER[1])
+                    quantize_score(ORDER[0], ((2, 3),))
+                    quantize_score(ORDER[1], ((2, 3),))
                     nc.vector.tensor_copy(out=gain_sb[:], in_=gain_raw[:, :, 0])
                     nc.vector.tensor_scalar(
                         out=minus_gain[:], in0=gain_raw[:, :, 0], scalar1=-1.0 / T, scalar2=None, op0=ALU.mult
                     )
 
-        weigh_slots(1)
+        weigh_slots(1, range(PACK))
+        if LATE == 5:
+            sort_slots(ORDER[3], 0)
+            sort_slots(ORDER[3], 1)
         correlate(ORDER[0], 0, 0, LAST)
         correlate(ORDER[0], 1, 0, LAST)
-        correlate(ORDER[1], 0, 0, LAST)
+        if not RUN16:
+            correlate(ORDER[1], 0, 0, LAST)
         quantize_sources(LAST, 0)
         quantize_last_score(ORDER[0])
         correlate(ORDER[0], 0, LAST, GROUPS)
         quantize_sources(LAST, 1)
         correlate(ORDER[0], 1, LAST, GROUPS)
         quantize_last_score(ORDER[1])
-        correlate(ORDER[1], 0, LAST, GROUPS)
+        correlate(ORDER[1], 0, 0 if RUN16 else LAST, GROUPS)
         correlate(ORDER[1], 1, 0, GROUPS)
         quantize_score(ORDER[2])
         quantize_last_score(ORDER[2])
+        weigh_score(nc.vector, ORDER[3], 2, LAST)
         both = (0, 1)
         for i in range(BLOCKS - 2):
             if i + 4 < BLOCKS:
@@ -446,7 +473,11 @@ def tile_infomax_relative_step_k6_kernel(
             finish(c, first)
             finish(c, 1 - first)
             add_diagonal(c)
-            if i >= 1:
+            if PAIR:
+                if i >= 2 and i % 2 == 0:
+                    turn_y(ORDER[i - 2], both, nc.scalar.copy)
+                    turn_y(ORDER[i - 1], both, nc.scalar.copy)
+            elif i >= 1:
                 turn_y(ORDER[i - 1], both, nc.scalar.copy)
             if i + 2 < BLOCKS:
                 correlate(ORDER[i + 2], 0, 0, GROUPS)
@@ -455,13 +486,22 @@ def tile_infomax_relative_step_k6_kernel(
             round_y(c, first, nc.scalar.copy)
             if i + 4 < BLOCKS:
                 weigh_score(nc.vector, ORDER[i + 4], 2, LAST)
-            if i >= 2:
+            if PAIR:
+                if i >= 3:
+                    quantize_y(ORDER[i - 3], both)
+                    if i % 2 == 0:
+                        store_codes(ORDER[i - 4], ORDER[i - 3] + 1)
+            elif i >= 2:
                 quantize_y(ORDER[i - 2], both)
                 if i % 2 == 1:
                     store_codes(ORDER[i - 3], ORDER[i - 2] + 1)
             if i + 3 < BLOCKS:
                 quantize_score(ORDER[i + 3])
                 quantize_last_score(ORDER[i + 3])
+        if PAIR:
+            turn_y(ORDER[-4], both, nc.scalar.copy)
+            quantize_y(ORDER[3], both)
+            store_codes(ORDER[2], ORDER[3] + 1)
         for c, copy in ((ORDER[-2], nc.scalar.copy), (ORDER[-1], nc.vector.tensor_copy)):
             first = c // (BLOCKS // HALVES)
             finish(c, first)

from contextlib import ExitStack

import concourse.mybir as mybir
from concourse.masks import make_identity

T, K, N = 2048, 512, 1024
FLOPS = 2 * T * 2 * K * N + 2 * T * N * N

F32 = mybir.dt.float32
BF16 = mybir.dt.bfloat16
I32 = mybir.dt.int32
U32 = mybir.dt.uint32
U8 = mybir.dt.uint8
FP8X4 = mybir.dt.float8_e4m3fn_x4
FP4X4 = mybir.dt.float4_e2m1fn_x4
ACT = mybir.ActivationFunctionType
ALU = mybir.AluOpType

P = 128
PACK = 4
GROUP = P * PACK
GROUPS = T // GROUP
BLOCKS = N // P
HALVES = N // GROUP
W_CHUNKS = ((0, 512), (512, 1024))
LAST = GROUPS - 1
W_TAGS = ("slots", "slots")
BUFS = {"phi": 8, "slots": 3}
LATE = 5
RUN16 = False
TURN0 = 2
SLOTNB = 1
FIRST = (2, 3, 0, 1, 4, 5, 6, 7)
PAIR = False
WARM0 = 16
WARM1 = 8
WARM2 = 8
ORDER = (2, 3, 4, 5, 6, 7, 0, 1)


def tile_infomax_relative_step_k6_kernel(
    tc, x, w, r, v_words, v_scales, left, right, gain, carry, out_0, out_1, out_2
):
    nc = tc.nc
    with ExitStack() as ctx:
        keep = ctx.enter_context(tc.tile_pool(name="keep", bufs=1))
        work = ctx.enter_context(tc.tile_pool(name="work", bufs=2))
        acc = ctx.enter_context(tc.psum_pool(name="acc", bufs=4 if RUN16 else 5))
        turn = ctx.enter_context(tc.psum_pool(name="turn", bufs=4 if RUN16 else 3))
        ctx.enter_context(tc.manual_schedule())

        ident = keep.tile([P, P], F32)
        make_identity(nc, ident[:])
        zeros = keep.tile([P, GROUP], BF16, align_bytes=64)
        nc.vector.memset(zeros[:], 0.0)
        v_plane = keep.tile([P, N], U8, align_bytes=64)
        nc.vector.memset(v_plane[:].bitcast(I32), 0)
        warm_codes = keep.tile([P, P], U32, align_bytes=64)
        warm_scales = keep.tile([P, P], U8, align_bytes=64)
        nc.vector.quantize_mx(out=warm_codes[:].bitcast(FP8X4), scales=warm_scales[:], in_=zeros[:])

        def warm_up(name, passes):
            bank = acc.tile([P, P], F32, name=name, tag="acc")
            for i in range(passes):
                nc.tensor.matmul_mx(
                    out=bank[:], lhsT=warm_codes[:].bitcast(FP8X4), lhsT_scale=warm_scales[:],
                    rhs=warm_codes[:].bitcast(FP8X4), rhs_scale=warm_scales[:], start=True, stop=True,
                )

        warm_up("warm0", WARM0)
        warm = keep.tile([P, 1], F32)
        nc.scalar.activation(out=warm[:], in_=ident[:, 0:1], func=ACT.Tanh)

        raw = {}

        def load_rows(name, src, g):
            tile = work.tile([P, PACK, K], BF16, name="raw_%s%d" % (name, g), tag="raw", bufs=5)
            nc.sync.dma_start(out=tile[:], in_=src[g * GROUP : (g + 1) * GROUP, :].rearrange("(p t) k -> p t k", t=PACK))
            raw[name, g] = tile

        w_raw = {}

        def load_w(i):
            lo, hi = W_CHUNKS[i]
            tile = work.tile([P, PACK, hi - lo], BF16, name="w_raw%d" % i, tag=W_TAGS[i], bufs=BUFS[W_TAGS[i]], align_bytes=64)
            nc.sync.dma_start(out=tile[:], in_=w.rearrange("(p j) n -> p j n", j=PACK)[:, :, lo:hi])
            w_raw[i] = tile

        load_rows("x", x, 0)
        load_w(0)
        load_rows("r", r, 0)
        v_codes = keep.tile([P, 2 * N], U8, align_bytes=64)
        nc.sync.dma_start(out=v_codes[:].bitcast(I32), in_=v_words[0].bitcast(I32))
        for q in range(4):
            nc.sync.dma_start(
                out=v_plane[32 * q : 32 * q + 4, :].bitcast(I32),
                in_=v_scales[0, 4 * q : 4 * q + 4, :].bitcast(I32),
            )
        right_sb = keep.tile([P, GROUPS, PACK], BF16)
        nc.sync.dma_start(out=right_sb[:], in_=right.rearrange("(g p t) -> p g t", p=P, t=PACK))
        load_w(1)
        left_sb = keep.tile([P, GROUPS, PACK], BF16)
        nc.sync.dma_start(out=left_sb[:], in_=left.rearrange("(g p t) -> p g t", p=P, t=PACK))
        load_rows("x", x, 1)
        load_rows("r", r, 1)
        load_rows("x", x, 2)

        w_sorted = {}
        w_codes = {}
        w_scales = {}

        def sort_w(i):
            lo, hi = W_CHUNKS[i]
            tile = work.tile([P, hi - lo, PACK], BF16, name="w_sorted%d" % i, tag=W_TAGS[i], bufs=BUFS[W_TAGS[i]], align_bytes=64)
            out = tile[:].rearrange("p (c i) j -> p c j i", i=4)
            in_ = w_raw[i][:].rearrange("p j (c i) -> p c j i", i=4)
            nc.vector.tensor_copy(out=out, in_=in_)
            w_sorted[i] = tile

        def quantize_w(i):
            lo, hi = W_CHUNKS[i]
            codes = keep.tile([P, hi - lo], U32, name="w_codes%d" % i, align_bytes=64)
            scales = keep.tile([P, hi - lo], U8, name="w_scales%d" % i, align_bytes=64)
            nc.vector.quantize_mx(
                out=codes[:].bitcast(FP8X4), scales=scales[:], in_=w_sorted[i][:].rearrange("p n j -> p (n j)")
            )
            for nb in range(lo // P, hi // P):
                cols = slice(nb * P - lo, (nb + 1) * P - lo)
                w_codes[nb] = codes[:, cols]
                w_scales[nb] = scales[:, cols]

        turned = {}
        in_codes = {}
        in_scales = {}

        def turn_rows(name, g, h):
            bank = turn.tile([P, 2, 2, P], F32, name="bank_%s%d%d" % (name, g, h), tag="turn")
            words = raw[name, g][:].rearrange("p t k -> p (t k)").bitcast(F32)
            for t in range(2):
                for u in range(2):
                    nc.tensor.transpose(bank[:, t, u, :], words[:, 256 * (2 * h + t) + u : 256 * (2 * h + t + 1) : 2], ident[:])
            if h == 0:
                turned[name, g] = work.tile([P, GROUP * PACK], BF16, name="turned_%s%d" % (name, g), tag="turned", bufs=2, align_bytes=64)
                in_codes[name, g] = work.tile([P, GROUP], U32, name="in_codes_%s%d" % (name, g), tag="in_codes", bufs=4, align_bytes=64)
                in_scales[name, g] = work.tile([P, GROUP], U8, name="in_scales_%s%d" % (name, g), tag="in_scales", bufs=4, align_bytes=64)
            nc.scalar.copy(
                out=turned[name, g][:, 2 * h * GROUP : 2 * (h + 1) * GROUP].bitcast(F32).rearrange("p (t m u) -> p t m u", t=2, u=2),
                in_=bank[:].rearrange("p t u m -> p t m u"),
            )

        def quantize_rows(name, g, lo, hi):
            cols = slice(2 * lo * P, 2 * hi * P)
            nc.vector.quantize_mx(
                out=in_codes[name, g][:, cols].bitcast(FP8X4), scales=in_scales[name, g][:, cols],
                in_=turned[name, g][:, 2 * lo * GROUP : 2 * hi * GROUP],
            )

        score = {}
        first_group = {}
        for nb in range(BLOCKS):
            first_group[nb] = 2 if nb in ORDER[-LATE:] else 0
            score[nb] = keep.tile([P, GROUPS - first_group[nb], P, PACK], F32, name="score%d" % nb)
        slot_score = {}
        for g in range(2):
            slot_score[g] = keep.tile([P, PACK, LATE, P], F32, name="slot_score%d" % g)
        z_banks = {}
        zr = {}
        zr_codes = {}
        zr_scales = {}

        def sources(g, nb):
            bank = acc.tile([P, PACK, P], F32, name="z%d%d" % (g, nb), tag="acc")
            for t in range(PACK):
                cols = slice(t * P, (t + 1) * P)
                nc.tensor.matmul_mx(
                    out=bank[:, t, :],
                    lhsT=in_codes["x", g][:, cols].bitcast(FP8X4), lhsT_scale=in_scales["x", g][:, cols],
                    rhs=w_codes[nb].bitcast(FP8X4), rhs_scale=w_scales[nb],
                    start=True, stop=False,
                )
                nc.tensor.matmul_mx(
                    out=bank[:, t, :],
                    lhsT=in_codes["r", g][:, cols].bitcast(FP8X4), lhsT_scale=in_scales["r", g][:, cols],
                    rhs=v_codes[:, 2 * nb * P : 2 * (nb + 1) * P].bitcast(FP4X4),
                    rhs_scale=v_plane[:, nb * P : (nb + 1) * P],
                    start=False, stop=True,
                )
            if g < first_group[nb]:
                nc.scalar.activation(out=slot_score[g][:, :, ORDER[-LATE:].index(nb), :], in_=bank[:], func=ACT.Tanh)
            else:
                nc.scalar.activation(
                    out=score[nb][:, g - first_group[nb], :, :], in_=bank[:].rearrange("p t n -> p n t"), func=ACT.Tanh
                )
            z_banks[g, nb] = bank

        def weigh_sources(g, nb):
            half, i = divmod(nb, BLOCKS // HALVES)
            if (g, half) not in zr:
                zr[g, half] = work.tile([P, GROUP, PACK], BF16, name="zr%d%d" % (g, half), tag="zr", bufs=3, align_bytes=64)
            nc.vector.tensor_tensor(
                out=zr[g, half][:, i * P : (i + 1) * P, :],
                in0=z_banks[g, nb][:].rearrange("p t n -> p n t"),
                in1=right_sb[:, g, :].unsqueeze(1).to_broadcast([P, P, PACK]),
                op=ALU.mult,
            )

        def quantize_sources(g, half):
            codes = keep.tile([P, GROUP], U32, name="zr_codes%d%d" % (g, half), align_bytes=64)
            scales = keep.tile([P, GROUP], U8, name="zr_scales%d%d" % (g, half), align_bytes=64)
            nc.vector.quantize_mx(
                out=codes[:].bitcast(FP8X4), scales=scales[:], in_=zr[g, half][:].rearrange("p n t -> p (n t)")
            )
            zr_codes[g, half] = codes
            zr_scales[g, half] = scales

        phi = {}
        phi_last = {}
        phi_codes = {}
        phi_scales = {}

        def phi_tile(c):
            if c not in phi:
                phi[c] = work.tile([P, LAST, P, PACK], BF16, name="phi%d" % c, tag="phi", bufs=BUFS["phi"], align_bytes=64)

        slot_phi = {}

        def weigh_slots(g, slots):
            if g not in slot_phi:
              slot_phi[g] = work.tile([P, PACK, LATE, P], BF16, name="slot_phi%d" % g, tag="slots", bufs=BUFS["slots"], align_bytes=64)
            for t in slots:
                nc.scalar.activation(
                    out=slot_phi[g][:, t, :, :], in_=slot_score[g][:, t, :, :], func=ACT.Copy, scale=left32[:, g, t : t + 1]
                )

        def sort_slots(c, g):
            phi_tile(c)
            nc.scalar.copy(
                out=phi[c][:, g, :, :].rearrange("p (n i) t -> p n t i", i=4),
                in_=slot_phi[g][:, :, ORDER[-LATE:].index(c), :].rearrange("p t (n i) -> p n t i", i=4),
            )

        def weigh_score(engine, c, lo, hi):
            phi_tile(c)
            engine.tensor_tensor(
                out=phi[c][:, lo:hi, :, :],
                in0=score[c][:, lo - first_group[c] : hi - first_group[c], :, :],
                in1=left_sb[:, lo:hi, :].unsqueeze(2).to_broadcast([P, hi - lo, P, PACK]),
                op=ALU.mult,
            )

        def weigh_last_score(c, tag, bufs):
            phi_last[c] = work.tile([P, P, PACK], BF16, name="phi_last%d" % c, tag=tag, bufs=bufs, align_bytes=64)
            nc.gpsimd.tensor_tensor(
                out=phi_last[c][:],
                in0=score[c][:, LAST - first_group[c], :, :],
                in1=left_sb[:, LAST, :].unsqueeze(1).to_broadcast([P, P, PACK]),
                op=ALU.mult,
            )

        def quantize_score(c, parts=((0, 2), (2, 3))):
          if c not in phi_codes:
            phi_codes[c] = work.tile([P, GROUPS * P], U32, name="phi_codes%d" % c, tag="phi_codes", bufs=4, align_bytes=64)
            phi_scales[c] = work.tile([P, GROUPS * P], U8, name="phi_scales%d" % c, tag="phi_scales", bufs=4, align_bytes=64)
          if True:
            flat = phi[c][:].rearrange("p g n t -> p (g n t)")
            for lo, hi in parts:
                nc.vector.quantize_mx(
                    out=phi_codes[c][:, lo * P : hi * P].bitcast(FP8X4), scales=phi_scales[c][:, lo * P : hi * P],
                    in_=flat[:, lo * GROUP : hi * GROUP],
                )

        def quantize_last_score(c):
            nc.vector.quantize_mx(
                out=phi_codes[c][:, LAST * P :].bitcast(FP8X4), scales=phi_scales[c][:, LAST * P :],
                in_=phi_last[c][:].rearrange("p n t -> p (n t)"),
            )

        c_banks = {}

        def correlate(c, half, lo, hi):
            if lo == 0:
                c_banks[c, half] = acc.tile([P, GROUP], F32, name="c%d%d" % (c, half), tag="acc")
            for g in range(lo, hi):
                cols = slice(g * P, (g + 1) * P)
                nc.tensor.matmul_mx(
                    out=c_banks[c, half][:],
                    lhsT=phi_codes[c][:, cols].bitcast(FP8X4), lhsT_scale=phi_scales[c][:, cols],
                    rhs=zr_codes[g, half][:].bitcast(FP8X4), rhs_scale=zr_scales[g, half][:],
                    start=(g == 0), stop=(g == LAST),
                )

        y = {}
        y_rows = {}
        carry_sb = {}

        def finish(c, half):
            if c not in y_rows:
                y_rows[c] = work.tile([P, N], F32, name="y%d" % c, tag="raw", bufs=5)
            y[c, half] = y_rows[c][:, half * GROUP : (half + 1) * GROUP]
            nc.vector.scalar_tensor_tensor(
                out=y[c, half], in0=c_banks[c, half][:], scalar=minus_gain[:, c : c + 1],
                in1=carry_sb[c // 2][:, c % 2, half * GROUP : (half + 1) * GROUP],
                op0=ALU.mult, op1=ALU.add,
            )

        def add_diagonal(c):
            half, i = divmod(c, BLOCKS // HALVES)
            block = y[c, half][:, i * P : (i + 1) * P]
            nc.vector.scalar_tensor_tensor(
                out=block, in0=ident[:], scalar=gain_sb[:, c : c + 1], in1=block, op0=ALU.mult, op1=ALU.add
            )
            nc.sync.dma_start(out=out_0[c * P : (c + 1) * P, :], in_=y_rows[c][:])

        y_sorted = {}
        y_turned = {}

        def round_y(c, half, copy):
            y_sorted[c, half] = work.tile([P, GROUP], BF16, name="y_sorted%d%d" % (c, half), tag="y_sorted", bufs=6)
            copy(
                out=y_sorted[c, half][:].rearrange("m (u p e) -> m u p e", u=2, e=2),
                in_=y[c, half].rearrange("m (p u e) -> m u p e", u=2, e=2),
            )

        def turn_y(c, halves, copy):
            bank = turn.tile([P, len(halves), 2, P], F32, name="bank_y%d%d" % (c, halves[0]), tag="turn")
            for i, half in enumerate(halves):
                words = y_sorted[c, half][:].bitcast(F32)
                for u in range(2):
                    nc.tensor.transpose(bank[:, i, u, :], words[:, u * P : (u + 1) * P], ident[:])
            tile = work.tile([P, len(halves) * GROUP], BF16, name="y_turned%d%d" % (c, halves[0]), tag="y_turned", bufs=4, align_bytes=64)
            copy(
                out=tile[:].bitcast(F32).rearrange("p (h m u) -> p h m u", h=len(halves), u=2),
                in_=bank[:].rearrange("p h u m -> p h m u"),
            )
            for i, half in enumerate(halves):
                y_turned[c, half] = tile[:, i * GROUP : (i + 1) * GROUP]

        y_scales = keep.tile([P, HALVES, N], U8, align_bytes=64)

        y_codes = keep.tile([P, HALVES, N], U32, align_bytes=64)

        def quantize_y(c, halves):
            for half in halves:
                nc.vector.quantize_mx(
                    out=y_codes[:, half, c * P : (c + 1) * P].bitcast(FP8X4),
                    scales=y_scales[:, half, c * P : (c + 1) * P],
                    in_=y_turned[c, half],
                )

        def store_codes(lo, hi):
            nc.sync.dma_start(
                out=out_1[:, :, lo * P : hi * P, :].rearrange("h p m t -> p h (m t)").bitcast(I32),
                in_=y_codes[:, :, lo * P : hi * P].bitcast(I32),
            )

        turn_rows("x", 0, 0)
        turn_rows("x", 0, 1)
        warm_up("warm1", WARM1)
        turn_rows("r", 0, 0)
        turn_rows("r", 0, 1)
        warm_up("warm2", WARM2)
        sort_w(0)
        quantize_rows("x", 0, 0, 2)
        quantize_w(0)
        quantize_rows("r", 0, 0, 1)
        quantize_rows("r", 0, 1, 2)
        sort_w(1)

        load_rows("r", r, 2)
        load_rows("x", x, LAST)
        gain_raw = keep.tile([P, BLOCKS, 2], BF16)

        def load_rest():
            load_rows("r", r, LAST)
            with nc.allow_non_contiguous_dma(reason="one gain to a partition"):
                nc.sync.dma_start(out=gain_raw[:, :, 0], in_=gain.rearrange("(c p) -> p c", p=P))
            for i in range(BLOCKS // 2):
                carry_sb[i] = keep.tile([P, 2, N], BF16, name="carry%d" % i)
                nc.sync.dma_start(
                    out=carry_sb[i][:], in_=carry[2 * i * P : 2 * (i + 1) * P, :].rearrange("(c p) n -> p c n", p=P)
                )

        left32 = keep.tile([P, GROUPS, PACK], F32)
        gain_sb = keep.tile([P, BLOCKS], F32)
        minus_gain = keep.tile([P, BLOCKS], F32)

        for g in range(GROUPS):
            turn_at = TURN0 if g == 0 else 0
            for nb in range(BLOCKS):
                block = FIRST[nb] if g == 0 else nb
                sources(g, block)
                weigh_sources(g, block)
                if g == 0:
                    if nb == 0:
                        weigh_score(nc.gpsimd, ORDER[0], g, g + 1)
                    if nb == 2:
                        quantize_w(1)
                    if nb == 4:
                        weigh_score(nc.gpsimd, ORDER[2], g, g + 1)
                        weigh_score(nc.gpsimd, ORDER[1], g, g + 1)
                elif nb in ORDER[:3]:
                    if g < LAST:
                        weigh_score(nc.gpsimd, nb, g, g + 1)
                    elif nb == ORDER[2]:
                        weigh_last_score(nb, "phi_late", 1)
                    else:
                        weigh_last_score(nb, "phi_early", 2)
                if nb == 0 and g > 0:
                    quantize_sources(g - 1, 0)
                    quantize_sources(g - 1, 1)
                if nb == 0 and g == 2:
                    quantize_score(ORDER[0], ((0, 2),))
                    quantize_score(ORDER[1], ((0, 2),))
                if nb == 3 and g == 0:
                    nc.vector.tensor_copy(out=left32[:], in_=left_sb[:])
                if nb == 4 and g == LAST:
                    weigh_slots(0, (2, 3))
                if nb == SLOTNB and g in (1, 2):
                    weigh_slots(0, (g - 1,))
                if LATE == 4 and nb == 0 and g in (1, 2):
                    weigh_score(nc.vector, ORDER[3], g - 1, g)
                if RUN16 and nb == turn_at and g < LAST:
                    for name in ("x", "r"):
                        turn_rows(name, g + 1, 0)
                        turn_rows(name, g + 1, 1)
                    for name in ("x", "r"):
                        quantize_rows(name, g + 1, 0, 2)
                    if g == 0:
                        load_rest()
                if not RUN16 and turn_at <= nb < turn_at + 2 and g < LAST:
                    name = ("x", "r")[nb - turn_at]
                    turn_rows(name, g + 1, 0)
                    turn_rows(name, g + 1, 1)
                    quantize_rows(name, g + 1, 0, 2)
                    if g == 0 and name == "x":
                        load_rest()
                if nb == 0 and g == LAST:
                    quantize_score(ORDER[0], ((2, 3),))
                    quantize_score(ORDER[1], ((2, 3),))
                    nc.vector.tensor_copy(out=gain_sb[:], in_=gain_raw[:, :, 0])
                    nc.vector.tensor_scalar(
                        out=minus_gain[:], in0=gain_raw[:, :, 0], scalar1=-1.0 / T, scalar2=None, op0=ALU.mult
                    )

        weigh_slots(1, range(PACK))
        if LATE == 5:
            sort_slots(ORDER[3], 0)
            sort_slots(ORDER[3], 1)
        correlate(ORDER[0], 0, 0, LAST)
        correlate(ORDER[0], 1, 0, LAST)
        if not RUN16:
            correlate(ORDER[1], 0, 0, LAST)
        quantize_sources(LAST, 0)
        quantize_last_score(ORDER[0])
        correlate(ORDER[0], 0, LAST, GROUPS)
        quantize_sources(LAST, 1)
        correlate(ORDER[0], 1, LAST, GROUPS)
        quantize_last_score(ORDER[1])
        correlate(ORDER[1], 0, 0 if RUN16 else LAST, GROUPS)
        correlate(ORDER[1], 1, 0, GROUPS)
        quantize_score(ORDER[2])
        quantize_last_score(ORDER[2])
        weigh_score(nc.vector, ORDER[3], 2, LAST)
        both = (0, 1)
        for i in range(BLOCKS - 2):
            if i + 4 < BLOCKS:
                sort_slots(ORDER[i + 4], 0)
                sort_slots(ORDER[i + 4], 1)
            if i + 3 < BLOCKS:
                weigh_last_score(ORDER[i + 3], "phi_late", 1)
            c = ORDER[i]
            first = c // (BLOCKS // HALVES)
            finish(c, first)
            finish(c, 1 - first)
            add_diagonal(c)
            if PAIR:
                if i >= 2 and i % 2 == 0:
                    turn_y(ORDER[i - 2], both, nc.scalar.copy)
                    turn_y(ORDER[i - 1], both, nc.scalar.copy)
            elif i >= 1:
                turn_y(ORDER[i - 1], both, nc.scalar.copy)
            if i + 2 < BLOCKS:
                correlate(ORDER[i + 2], 0, 0, GROUPS)
                correlate(ORDER[i + 2], 1, 0, GROUPS)
            round_y(c, 1 - first, nc.scalar.copy)
            round_y(c, first, nc.scalar.copy)
            if i + 4 < BLOCKS:
                weigh_score(nc.vector, ORDER[i + 4], 2, LAST)
            if PAIR:
                if i >= 3:
                    quantize_y(ORDER[i - 3], both)
                    if i % 2 == 0:
                        store_codes(ORDER[i - 4], ORDER[i - 3] + 1)
            elif i >= 2:
                quantize_y(ORDER[i - 2], both)
                if i % 2 == 1:
                    store_codes(ORDER[i - 3], ORDER[i - 2] + 1)
            if i + 3 < BLOCKS:
                quantize_score(ORDER[i + 3])
                quantize_last_score(ORDER[i + 3])
        if PAIR:
            turn_y(ORDER[-4], both, nc.scalar.copy)
            quantize_y(ORDER[3], both)
            store_codes(ORDER[2], ORDER[3] + 1)
        for c, copy in ((ORDER[-2], nc.scalar.copy), (ORDER[-1], nc.vector.tensor_copy)):
            first = c // (BLOCKS // HALVES)
            finish(c, first)
            finish(c, 1 - first)
            add_diagonal(c)
            round_y(c, 1 - first, copy)
            round_y(c, first, copy)
        turn_y(ORDER[-3], both, nc.scalar.copy)
        turn_y(ORDER[-2], both, nc.scalar.copy)
        quantize_y(ORDER[-4], both)
        quantize_y(ORDER[-3], both)
        store_codes(ORDER[-4], ORDER[-3] + 1)
        turn_y(c, (1 - first,), nc.scalar.copy)
        turn_y(c, (first,), nc.vector.tensor_copy)
        quantize_y(ORDER[-2], both)
        store_codes(ORDER[-2], ORDER[-2] + 1)
        quantize_y(c, (1 - first,))
        quantize_y(c, (first,))
        store_codes(c, c + 1)
        for q in range(4):
            (nc.sync, nc.scalar)[q % 2].dma_start(
                out=out_2[:, 4 * q : 4 * q + 4, :].rearrange("h r m -> r h m").bitcast(I32),
                in_=y_scales[32 * q : 32 * q + 4, :, :].bitcast(I32),
            )
